import numpy as np, ml_dtypes
CORES = [2,6,10,14,18,22,26,30]
N = 8
BF = ml_dtypes.bfloat16
def gentries(a):
    return np.ascontiguousarray(a.reshape(8, 16, -1).transpose(0, 2, 1)).reshape(8, -1)
def gtable(e):
    e = np.asarray(e); return np.ascontiguousarray(e.reshape(8, -1, 16).transpose(0, 2, 1)).reshape(128, -1).astype(np.int32)
R0, P0, S, L, RO = 8192, 576, 16, 13, 2
P = P0 + RO * S; R = R0 + RO * (N - 1) * S
def counts(rng, share):
    return np.where(rng.random((N, 8, P0)) < share, rng.integers(L, 17, (N, 8, P0)), rng.integers(1, L, (N, 8, P0)))
def world(rng, cnt):
    post = rng.integers(0, R0, (N, 8, P0, 16)); home = np.full((N, 8, R0), 65535)
    on = np.argsort(rng.random((N, 8, P0, 16)), axis=-1) < cnt[..., None]
    for q in range(N):
        for g in range(8):
            ix = np.flatnonzero(on[q, g])[:R0]; c = rng.permutation(R0); n = len(ix)
            post[q, g].reshape(-1)[ix] = c[:n]; home[q, g, c[:n]] = ix
            if n: home[q, g, c[n:]] = np.where(rng.random(R0 - n) < 0.5, 65535, ix[rng.integers(0, n, R0 - n)])
    cl = rng.integers(0, 24, (N, 8, P0)); pr = rng.integers(40, 200, (8, 24, 14)); gi = np.arange(8)[None, :, None]
    at = np.minimum(home >> 4, P0 - 1)
    kc = np.where(home == 65535, rng.integers(0, 24, home.shape), np.take_along_axis(cl, at, 2))
    x = np.clip(pr[gi, kc] + rng.integers(-40, 41, (N, 8, R0, 14)), 0, 255)
    cen = rng.integers(0, 256, (N, 8, P0, 16)); cen[..., :14] = pr[gi, cl] + rng.integers(-16, 17, (N, 8, P0, 14))
    m = N * P0; w = m // 24; od = np.argsort(cl.transpose(1, 0, 2).reshape(8, m) + rng.random((8, m)), axis=1); pos = np.argsort(od, axis=1)
    z = np.take_along_axis(od, ((pos[:, :, None] + rng.integers(-w, w + 1, (8, m, 16))) % m).reshape(8, 16 * m), 1)
    near = (P * (z // P0) + z % P0).reshape(8, N, P0, 16).transpose(1, 0, 2, 3)
    near = np.where(rng.random(near.shape) < 0.15, rng.integers(0, N * P, near.shape), near)
    sl = 16 * at[:, :, None, :] + rng.integers(0, 16, (N, 8, RO, R0))
    ab = np.take_along_axis(post.reshape(N, 8, 16 * P0), sl.reshape(N, 8, RO * R0), 2).reshape(N, 8, RO, R0); u = rng.random(ab.shape)
    ab = np.where(u < 0.3, np.arange(R0), np.where(u < 0.5, rng.integers(0, R, ab.shape), ab))
    return {"x": x, "home": home, "cen": cen, "post": post, "near": near, "ab": ab}
def pack(d):
    h = d["home"][..., None]; v = np.concatenate([d["x"], h >> 8, h & 255], axis=-1).astype(np.float32)
    def turn(a): return np.ascontiguousarray(a.transpose(0, 1, 3, 2)).reshape(N, 128, -1)
    return {"rec": turn(v).astype(BF), "post": turn(d["post"]).astype(np.int32), "cen": turn(d["cen"].astype(np.float32)).astype(BF), "near": turn(d["near"]).astype(np.int32),
            "absorb": np.stack([gtable(a.reshape(8, -1)) for a in d["ab"]])}
def setup_inputs(rng):
    return pack(world(rng, counts(rng, rng.choice(np.array([0.2, 0.4, 0.6]), (N, 8, 1)))))
def setup_inputs_room(rng):
    nf = rng.choice(np.array([0, 1, S - 1, S, S + 1, 3 * S]), (N, 8)); nf[0] = (S, S + 1, S - 1, 0, 1, 3 * S, S, 2 * S); nf[1, 0] = S
    fm = np.argsort(rng.random((N, 8, P0)), axis=-1) < nf[..., None]
    cnt = np.where(fm, rng.choice(np.array([L, 16]), fm.shape), np.where(rng.random(fm.shape) < 0.5, L - 1, rng.integers(1, L, fm.shape)))
    d = world(rng, cnt); d["x"][:, 0] = rng.integers(128, 256, (N, R0, 14)); d["cen"][:, 0, :, :14] = 0
    fp = np.flatnonzero(fm[1, 0]); fq = np.flatnonzero(~fm[0, 0])
    d["near"][0, 0, fq] = (P + fp[np.arange(len(fq)) % S])[:, None]
    return pack(d)
def setup_inputs_ties(rng):
    cnt = counts(rng, 0.5); cnt[:, :, :6] = 16
    d = world(rng, cnt); d["x"] = rng.integers(0, 3, (N, 8, R0, 14)); d["cen"][..., :14] = rng.integers(0, 3, (N, 8, P0, 14))
    d["x"][:, 0] = 7; d["cen"][:, 0, :, :14] = np.where(rng.random((N, P0, 1)) < 0.5, 7, rng.integers(5, 9, (N, P0, 14)))
    d["x"][:, 2] *= rng.random((N, R0, 1)) < 0.5; d["cen"][:, 2, :, :14] = rng.integers(5, 9, (N, P0, 14))
    d["ab"][:, :4] = np.arange(R0)
    d["near"][:, 1::2] = P * rng.integers(0, N, (N, 4, P0, 16)) + rng.integers(0, 6, (N, 4, P0, 16))
    return pack(d)
def setup_inputs_ends(rng):
    q = rng.permutation(N); cnt = counts(rng, 0.3); cnt[q[0]] = rng.integers(0, L, (8, P0)); cnt[q[1]] = L
    ch = rng.permutation(P0)[:5]; cnt[:, 3] = rng.integers(1, L, (N, P0)); cnt[:, 3, ch] = 16
    cnt[:, 4] = rng.integers(1, L, (N, P0)); cnt[:, 4, 0] = 16; cnt[:, 4, P0 - 1] = L
    d = world(rng, cnt); ab = d["ab"]; near = d["near"]; d["cen"][:, 3, :, :14] = 0
    ab[:, 1] = rng.choice(np.array([0, R0 - 1]), (N, RO, R0)); ab[:, 2] = rng.integers(R0, R, (N, RO, R0)); ab[:, 5] = rng.integers(0, R0, (N, 1, 1)); ab[:, 3] = np.arange(R0)
    near[:, 4] = P * rng.integers(0, N, (N, P0, 16)) + rng.choice(np.array([0, P0 - 1, P0, P - 1]), (N, P0, 16))
    near[:, 3] = P * rng.integers(0, N, (N, P0, 16)) + np.where(rng.random((N, P0, 16)) < 0.5, P0 + rng.integers(0, 5, (N, P0, 16)), ch[rng.integers(0, 5, (N, P0, 16))])
    for a in range(N):
        s = d["post"][a, 3, ch]; d["x"][a, 3, s[:, 0]] = 0; d["x"][a, 3, s[:, 1:].reshape(-1)] = rng.integers(200, 256, (75, 14))
    return pack(d)
def setup_inputs_sharp(rng):
    d = world(rng, counts(rng, 0.4)); E = N * S - 32; n = P0 - S; i = np.arange(n)
    tg = np.where(i < n - 32, i % E, E + i - (n - 32))
    for g in range(0, 8, 2):
        fs = [np.sort(rng.permutation(P0)[:S]) for q in range(N)]; to = np.concatenate([P * q + fs[q] for q in range(N)])
        for q in range(N):
            fp = fs[q]; fq = np.setdiff1d(np.arange(P0), fp); po = d["post"][q, g]
            dull = (rng.random(n) < 0.5) & ((i < E) | ((i >= 2 * E) & (i < n - 32)))
            z = int(np.flatnonzero(tg == q * S)[0]); dull[z] = False
            cnt = np.zeros(P0, np.int64); cnt[fp] = rng.integers(L, 16, S); cnt[fq] = rng.integers(1, 5, n); cnt[fq[z]] = 1
            key = rng.random((P0, 16)); key[fp, 0] = 2
            on = np.argsort(np.argsort(key, axis=1), axis=1) < cnt[:, None]
            ix = np.flatnonzero(on); m = len(ix); c = 1 + rng.permutation(R0 - 1); dead = c[m:]; low = dead[:len(dead) // 2]; high = dead[len(dead) // 2:]
            po[fp] = rng.choice(high, (S, 16)); po[fq] = rng.choice(low, (n, 16))
            po[on] = c[:m]; po[fq[z], int(np.argmax(on[fq[z]]))] = 0
            h = np.where(rng.random(R0) < 0.5, 65535, ix[rng.integers(0, m, R0)]); h[po[on]] = ix; d["home"][q, g] = h
            x = rng.integers(130, 201, (R0, 14)); x[low] = 0; x[high] = 255
            e = fp[::2]; x[po[e][on[e]]] = 0
            e = fp[1::2]; s = po[e][on[e]]; x[s] = rng.integers(0, 3, (len(s), 14))
            e = fq[~dull]; x[po[e][on[e]]] = 127
            d["x"][q, g] = x; d["cen"][q, g, fq, :14] = 255; d["ab"][q, g, 0] = np.arange(R0)
            d["near"][q, g, fq] = np.where(np.arange(16) < rng.integers(0, 15, (n, 1)), (P * q + fq)[:, None], to[tg][:, None])
    return pack(d)
def setup_inputs_spread(rng):
    d = world(rng, counts(rng, rng.random((N, 8, 1))))
    d["x"] = np.minimum((np.exp2(8 * rng.random((N, 8, R0, 1))) * rng.random((N, 8, R0, 14))).astype(np.int64), 255)
    d["cen"] = rng.integers(0, 256, (N, 8, P0, 16)) >> rng.integers(0, 8, (N, 8, P0, 1))
    d["near"] = rng.integers(0, N * P, (N, 8, P0, 16)); d["ab"] = rng.integers(0, R, (N, 8, RO, R0))
    return pack(d)
def check_inputs(d):
    bad = []
    for k, hi in (("rec", 255), ("cen", 255), ("post", R0 - 1), ("near", N * P - 1), ("absorb", R - 1)):
        v = np.asarray(d[k]).astype(np.float64)
        if not (np.min(v) >= 0 and np.max(v) <= hi) or np.any(v != np.floor(v)): bad.append("range of " + k)
    v = np.asarray(d["rec"]).astype(np.float64).reshape(N, 8, 16, R0); h = v[:, :, 14] * 256 + v[:, :, 15]
    if np.any((h >= 16 * P0) & (h != 65535)): bad.append("homes of rec")
    return bad
def reference(rec, post, cen, near, absorb):
    w = rec.astype(np.float32).astype(np.int32).reshape(N, 8, 16, R0)
    x = np.zeros((N, 8, 14, R), np.int32); x[..., :R0] = w[:, :, :14]
    home = np.full((N, 8, R), 65535, np.int64); home[..., :R0] = w[:, :, 14] * 256 + w[:, :, 15]
    po = np.zeros((N, 8, P, 16), np.int64); po[:, :, :P0] = post.reshape(N, 8, 16, P0).transpose(0, 1, 3, 2)
    ne = np.zeros((N, 8, P, 16), np.int64); ne[:, :, :P0] = near.reshape(N, 8, 16, P0).transpose(0, 1, 3, 2)
    ce = np.zeros((N, 8, 14, P), np.int32); ce[..., :P0] = cen.astype(np.float32).astype(np.int32).reshape(N, 8, 16, P0)[:, :, :14]
    al = np.stack([gentries(a) for a in absorb]).astype(np.int64).reshape(N, 8, RO, R0)
    for t in range(RO):
        new = P0 + S * t
        for q in range(N): x[q, :, :, :R0] = np.maximum(x[q, :, :, :R0], np.take_along_axis(x[q], al[q, :, t][:, None, :], 2))
        live = (np.take_along_axis(home, po.reshape(N, 8, 16 * P), 2) == np.arange(16 * P)).reshape(N, 8, P, 16)
        full = (np.add.reduce(live.astype(np.int64), axis=3) >= L).astype(np.int64)
        num = np.add.accumulate(full, axis=2) - full; sp = (full == 1) & (num < S)
        b = np.zeros((N, 8, S, 14), np.int32); row = np.zeros((N, 8, S), np.int64)
        for q in range(N):
            for g in range(8):
                for k, p in enumerate(np.flatnonzero(sp[q, g])):
                    f = new + k; ix = po[q, g, p].copy(); v = x[q, g][:, ix]; on = live[q, g, p]
                    va = v[:, np.argmax(on)]; da = np.add.reduce(np.abs(v - va[:, None]), axis=0)
                    vb = v[:, np.argmax(np.where(on, da, -1))]; db = np.add.reduce(np.abs(v - vb[:, None]), axis=0)
                    go = on & (db < da)
                    po[q, g, f] = ix; ne[q, g, f] = ne[q, g, p]; ce[q, g, :, p] = va; ce[q, g, :, f] = vb
                    home[q, g, ix[go]] = 16 * f + np.flatnonzero(go)
                    b[q, g, k] = vb; row[q, g, k] = np.argmin(go)
        tab = np.where(sp, num + S * np.arange(N)[:, None, None], -1).transpose(1, 0, 2).reshape(8, N * P)
        mov = np.full((N, 8, N * S), -1, np.int64)
        for q in range(N):
            tj = np.take_along_axis(tab, ne[q].reshape(8, 16 * P), 1).reshape(8, P, 16)
            tg = np.take_along_axis(tj, np.argmax(tj >= 0, axis=2)[:, :, None], 2)[:, :, 0]
            for g in range(8):
                Q = np.flatnonzero((tg[g] >= 0) & ~sp[q, g]); v = x[q, g][:, po[q, g, Q]]
                vb = b[:, g].reshape(N * S, 14).T[:, tg[g, Q]]
                gain = np.add.reduce(np.abs(v - ce[q, g][:, Q][:, :, None]), axis=0) - np.add.reduce(np.abs(v - vb[:, :, None]), axis=0)
                gain = np.where(live[q, g, Q], gain, 0); m = np.argmax(gain, axis=1); ok = np.any(gain > 0, axis=1)
                Q = Q[ok]; m = m[ok]; u, i = np.unique(tg[g, Q], return_index=True)
                mov[q, g, u] = po[q, g, Q[i], m[i]]
        for r in range(N):
            win = mov[r, :, r * S:(r + 1) * S].copy()
            for o, q in enumerate([a for a in range(N) if a != r]):
                c = mov[q, :, r * S:(r + 1) * S]; e = R0 + ((N - 1) * t + o) * S
                x[r, :, :, e:e + S] = np.where((c >= 0)[:, None, :], np.take_along_axis(x[q], np.maximum(c, 0)[:, None, :], 2), 0)
                gg, kk = np.nonzero(c >= 0); home[q, gg, c[gg, kk]] = 65535
                win = np.where((win < 0) & (c >= 0), e + np.arange(S), win)
            gg, kk = np.nonzero(win >= 0); m = row[r, gg, kk]
            home[r, gg, win[gg, kk]] = 16 * (new + kk) + m; po[r, gg, new + kk, m] = win[gg, kk]
    hh = np.stack([home >> 8, home & 255], axis=2)
    ya = np.concatenate([x[..., R0:], hh[..., R0:].astype(np.int32)], axis=2).reshape(N, 128, R - R0)
    return {"ypost": np.ascontiguousarray(po.transpose(0, 1, 3, 2)).reshape(N, 128, P).astype(np.float32),
            "yh": hh[..., :R0].reshape(N, 16, R0).astype(np.float32).astype(BF), "ya": ya.astype(np.float32).astype(BF)}

import comms_topo
from concourse.bass import DstId, RemoteDMATransfer
from concourse.mybir import AluOpType as A, AxisListType as AX, ActivationFunctionType as AF

XW = 8704
PW = 736
CH = [[(0, 224), (224, 448), (448, 576)], [(0, 224), (224, 448), (448, 608)]]
SCRATCH = {}
for _d, _l in [("bfloat16", "REC:8704 X1:8704 X2:8704 V:9728 MC0:3584 MC1:3584 MB0:3584 MB1:3584 HG:9728 TAB0:4992 TAB1:4992 PL:2048 PLF:2048 PLN:2048 PLH:2048 "
                "BD:128 D128:128 D16:16 TRI:128 WM:128 R15:128 BDm:128 CW:128 BW:128 CV:128 HV0:256 HV1:256 C255:128 RST:224 ONE:224 ZER:224 LV:736 LVN:736 CIN:576 C:736 "
                "BT0:144 BT1:144 ARR0:112 ARR1:112 BA:4096 BL:4096 E:1792 SC:1792"),
               ("float32", "BDf:128 D16f:16 R15f:128 M30:16 TC:8 TCN:8 NJC:8 DM:16 K16:16 CK:64 IOJ:256 IOG:128 IOM:128 IOS:608 IOQ:8 SLOT:608 CUM:608 "
                "RZ0:32 RZ1:32 RV0:32 RV1:32 POSTF:736 K1:736 ST:736 FT:2048 FLT:768 KT:224 SG:224"),
               ("int32", "PI:8 POSTI:576 NEI:736 ABI:1024"), ("uint16", "RL8:8 ABU:1024 POSTU:608 NLU:608 UT:1024")]:
    for _x in _l.split():
        SCRATCH[_x.split(":")[0]] = ("sbuf", [128, int(_x.split(":")[1])], _d)
for _i in range(8):
    SCRATCH["q%d" % _i] = ("psum", [128, 512], "float32")
NDMA = 22
SEMAPHORES = ["V", "S", "P", "G", "LS"] + ["d%d" % i for i in range(NDMA)] + [m + str(t) for m in ("mz", "mb", "mv", "ma") for t in (0, 1)]
EPS, WAKE, MSG = 50, 100, 4200
FLEX = 5


def rank_program(g, core, T, topo):
    rank = T.rank_of(core)
    if rank is None:
        return
    eng = {"V": g.vector, "S": g.scalar, "P": g.tensor, "G": g, "Y": g.sync}
    nodes, wlist, rlist, bank, top = [], {}, {}, {}, {}

    def R(name, a=0, b=None, st=1):
        return (name, a, SCRATCH[name][1][1] if b is None else b, st)

    def I(win, off):
        return ("I", win, off)

    def cols(r, a, b, st=1):
        return (r[0], r[1] + a, r[1] + b, st)

    def ap(r):
        if not isinstance(r, tuple):
            return r
        if r[0] == "I":
            return ap(r[1]).indirect(ap(r[2]))
        return T[r[0]][:, r[1]:r[2]] if r[3] == 1 else T[r[0]][:, r[1]:r[2]:r[3]]

    def wide(r):
        return 16 * (r[2][2] - r[2][1]) if r[0] == "I" else (r[2] - r[1] + r[3] - 1) // r[3]

    def two(*rs):
        return all([SCRATCH[r[0]][2] in ("bfloat16", "uint16") for r in rs if isinstance(r, tuple) and r[0] != "I" and wide(r) > 1])

    def meet(x, y):
        if x[1] >= y[2] or y[1] >= x[2]:
            return False
        return not (x[3] > 1 and x[3] == y[3] and (x[1] - y[1]) % x[3])

    def node(e, call, outs, ins, cost, lat=0, kind="c", src=None, amount=1, after=()):
        k = len(nodes)
        deps = set(after)
        w, rd = [], []
        for o in outs:
            if o[0] == "I":
                w.append(o[1])
                rd.append(o[2])
            else:
                w.append(o)
        for i in ins:
            if isinstance(i, tuple):
                rd += [i[1], i[2]] if i[0] == "I" else [i]
        for wr, rs in ((False, rd), (True, w)):
            for r in rs:
                b = r[0]
                if b[0] == "q":
                    old = bank.get(b, [])
                    for (j, r2, wr2, e2) in old:
                        if j != k and (e2 != e or e == "P" or len(e) > 1 or ((wr or wr2) and meet(r, r2))):
                            deps.add(j)
                    if e == "P" or (wr and all([r[1] <= x[1][1] and x[1][2] <= r[2] and r[3] == 1 for x in old])):
                        old = []
                    bank[b] = old + [(k, r, wr, e)]
                    continue
                for j, r2 in wlist.get(b, []):
                    if j != k and meet(r, r2):
                        deps.add(j)
                if wr:
                    for j, r2 in rlist.get(b, []):
                        if j != k and meet(r, r2):
                            deps.add(j)
                    for L in (wlist, rlist):
                        L[b] = [x for x in L.get(b, []) if x[0] == k or not (r[3] == 1 and r[1] <= x[1][1] and x[1][2] <= r[2])]
                    wlist[b] = wlist[b] + [(k, r)]
                else:
                    rlist[b] = rlist.get(b, []) + [(k, r)]
        nodes.append({"e": e, "call": call, "deps": deps, "cost": cost, "lat": lat, "kind": kind, "src": src, "amount": amount})
        return k

    def schedule():
        n = len(nodes)
        prio, users, left = [0] * n, [[] for _ in nodes], [len(x["deps"]) for x in nodes]
        for k in range(n - 1, -1, -1):
            x = nodes[k]
            prio[k] += x["cost"] + x["lat"]
            for d in x["deps"]:
                prio[d] = max(prio[d], prio[k] + WAKE)
                users[d].append(k)
        free = {e: 0 for e in eng}
        ready = {e: [] for e in eng}
        order = []

        def done(k, t):
            nodes[k]["end"] = t
            for u in users[k]:
                left[u] -= 1
                if left[u] == 0:
                    offer(u)

        def offer(u):
            x = nodes[u]
            t = max([0] + [nodes[d]["end"] + WAKE for d in x["deps"]])
            if x["kind"] == "a":
                order.append(u)
                done(u, t + x["lat"])
            else:
                x["ready"] = t
                for e in x["e"]:
                    ready[e].append(u)
        for k in range(n):
            if not nodes[k]["deps"] and "ready" not in nodes[k]:
                offer(k)
        while len(order) < n:
            pick, ok = None, {}
            for e in eng:
                ok[e] = ready[e]
                if e == "V" and len([k for k in ready["S"] if len(nodes[k]["e"]) > 1]) < FLEX:
                    ok[e] = [k for k in ready[e] if len(nodes[k]["e"]) == 1]
                if ok[e]:
                    s = min([max(free[e], nodes[k]["ready"]) for k in ok[e]])
                    if pick is None or s < pick[0]:
                        pick = (s, e)
            s, e = pick
            k = max([k for k in ok[e] if max(free[e], nodes[k]["ready"]) <= s + EPS], key=lambda k: (prio[k], -k))
            x = nodes[k]
            for f in x["e"]:
                ready[f].remove(k)
            x["e"] = e
            s = max(free[e], x["ready"])
            free[e] = s + x["cost"]
            order.append(k)
            done(k, free[e] + x["lat"])
        return order

    def emit():
        seq, know, clocks, total = {}, {e: {} for e in eng}, {}, {}
        for k in schedule():
            x = nodes[k]
            if x["kind"] == "a":
                x["num"], x["amt"], clocks[(x["src"], 1)] = 1, x["amount"], {}
                total[x["src"]] = x["amount"]
                continue
            e = x["e"]
            need = {}
            for d in x["deps"]:
                y = nodes[d]
                if y["kind"] == "r" or (e == "P" and y["e"] == "P"):
                    continue
                need[y["src"]] = max(need.get(y["src"], (0, 0)), (y["num"], y["num"] * y["amt"]))
            for s, (num, val) in sorted(need.items()):
                if know[e].get(s, 0) < num:
                    eng[e].wait_ge(T.sem[s], val)
                    for c, v in clocks[(s, num)].items():
                        know[e][c] = max(know[e].get(c, 0), v)
                    know[e][s] = num
            if x["kind"] == "r":
                x["call"](e)
                total["LS"] = total.get("LS", 0) + x["amount"]
                continue
            if x["kind"] == "c":
                x["src"] = e
                seq[e] = seq.get(e, 0) + 1
                x["num"], x["amt"] = seq[e], 1
            else:
                x["num"], x["amt"] = 1, 16
            x["call"](e).then_inc(T.sem[x["src"]], x["amt"])
            total[x["src"]] = x["num"] * x["amt"]
            clocks[(x["src"], x["num"])] = dict(know[e])
            clocks[(x["src"], x["num"])][x["src"]] = x["num"]
        for s, v in sorted(total.items()):
            g.wait_ge(T.sem[s], v)

    def vcost(n, f):
        return max(64, n * f) + 30

    def fill(o, c):
        node("V", lambda e: g.vector.memset(ap(o), c), [o], [], vcost(wide(o), 0.5 if two(o) else 1))

    def vc(o, i):
        n = wide(i) if o[0] == "I" else wide(o)
        c = 50 + 3.5 * n if o[0] == "I" else 80 + 1.5 * n if i[0] == "I" else vcost(n, 0.5 if two(o, i) else 1)
        node("V", lambda e: g.vector.tensor_copy(ap(o), ap(i)), [o], [i], c)
        return o

    def tt(o, a, b, f):
        n = wide(o)
        c = 80 + 1.5 * n if a[0] == "I" else vcost(n, 1 if "q" in (a[0][0], b[0][0]) else 2)
        node("V", lambda e: g.vector.tensor_tensor(ap(o), ap(a), ap(b), f), [o], [a, b], c)
        return o

    def ts(o, a, s1, f1, s2=None, f2=None):
        if f2 is None:
            call = lambda e: g.vector.tensor_scalar(ap(o), ap(a), ap(s1), None, f1)
        else:
            call = lambda e: g.vector.tensor_scalar(ap(o), ap(a), ap(s1), ap(s2), f1, f2)
        node("V", call, [o], [a, s1, s2], vcost(wide(o), 0.5 if two(o, a) else 1))
        return o

    def red(o, i, f):
        node("V", lambda e: g.vector.tensor_reduce(ap(o), ap(i), AX.X, f), [o], [i], vcost(wide(i), 1))
        return o

    def scan(o, a, b, init, f0, f1):
        node("V", lambda e: g.vector.tensor_tensor_scan(ap(o), ap(a), ap(b), ap(init), f0, f1), [o], [a, b, init], vcost(wide(o), 0.5 if two(o, a, b) else 1))
        return o

    def turn(o, i):
        node("V", lambda e: g.vector.transpose(ap(o), ap(i)), [o], [i], vcost(wide(o), 1))
        return o

    def act(o, i, f=AF.Copy, **kw):
        k2 = {k: ap(v) for k, v in kw.items()}
        node("S", lambda e: g.scalar.activation(ap(o), ap(i), f, **k2), [o], [i] + list(kw.values()), 100 + wide(o) * (1.5 if i[0] == "I" else 1))
        return o

    def either(o, i):
        n = wide(o)
        node("VS", lambda e: g.vector.tensor_copy(ap(o), ap(i)) if e == "V" else g.scalar.activation(ap(o), ap(i), AF.Copy), [o], [i], 90 + (1.5 if i[0] == "I" else 1) * n)
        return o

    def mm(o, l, r, start=True, stop=True):
        node("P", lambda e: g.tensor.matmul(ap(o), ap(l), ap(r), start, stop), [o], [l, r], max(64, wide(o)) * (1 if two(l) else 4))
        return o

    def iota(o, pat, mult=0, after=()):
        kw = {} if SCRATCH[o[0]][2] == "int32" else {"allow_small_or_imprecise_dtypes": True}
        return node("G", lambda e: g.iota(ap(o), pat, 0, mult, **kw), [o], [], 130 + 2 * wide(o), 0, "c", None, 1, after)

    def dma(e, out, in_, outs, ins, lat):
        src = "d%d" % top.get("d", 0)
        top["d"] = top.get("d", 0) + 1
        node(e, lambda e: eng[e].dma_start(out, in_), outs, ins, 60, lat, "d", src)

    def dests():
        return [d for d in T.cores if d != core]

    def ident(d):
        a = topo.addr(d)
        return DstId(rid=a[0], pnc=a[1])

    lanes = [i for i in topo.engines(core, dests()[0]) if all([i in topo.engines(core, d) for d in dests()])][:8]

    def arrive(sem, cnt, outs, sent):
        node("G", None, outs, [], 0, MSG, "a", sem, cnt, [sent])

    def send_all(src, sem, dst, lands):
        mask = sum([1 << i for i in lanes])
        k = node("G", lambda e: g.remote_dma_fused([RemoteDMATransfer(dst_ids=[ident(d) for d in dests()], dma_engine_mask=mask, remote_sem=T.sem[sem], srcs=[ap(src)],
                                                                      dsts=[ap(dst) for d in dests()])], local_sem=T.sem.LS), [], [src], 1000, 0, "r", None, len(lanes))
        arrive(sem, 7 * len(lanes), lands, k)
        return k

    def send_each(src, sem, dst, lands):
        ds = dests()
        k = node("G", lambda e: g.remote_dma_fused([RemoteDMATransfer(dst_ids=[ident(d)], dma_engine_mask=1 << lanes[i], remote_sem=T.sem[sem], srcs=[ap(src(d))], dsts=[ap(dst(d))])
                                                    for i, d in enumerate(ds)], local_sem=T.sem.LS), [], [src(d) for d in ds], 1000, 0, "r", None, len(ds))
        arrive(sem, 7, lands, k)

    def spread(o, pl, src, n):
        h = [0, n] if n < 128 else [0, 112, n] if n > 128 else [0, 64, n]
        for x, y in zip(h[:-1], h[1:]):
            for m in range(16):
                i = src(m)
                mm(cols(o, x, y), R(pl, 128 * m, 128 * m + 128), (i[0], i[1] + x * i[3], min(i[2], i[1] + y * i[3]), i[3]), m == 0, m == 15)

    def arena(name, ring):
        def new(n):
            w = (n + 15) // 16 * 16
            a = top.get(name, 0)
            if a + w > SCRATCH[name][1][1]:
                assert ring, name
                a = 0
            top[name] = a + w
            return R(name, a, a + n)
        return new
    F, B, U, FL, BL = arena("FT", True), arena("BA", True), arena("UT", False), arena("FLT", False), arena("BL", False)

    dma("S", T.POSTI[:], T.post[:], [R("POSTI")], [], 3000)
    dma("Y", T.REC[:, 0:8192], T.rec[:], [R("REC", 0, 8192)], [], 9000)
    dma("S", T.ABI[:, 0:512], T.absorb[:, 0:512], [R("ABI", 0, 512)], [], 4000)
    dma("Y", T.V[:, 0:4096], T.rec[:, 0:4096], [R("V", 0, 4096)], [], 12000)
    dma("S", T.NEI[:, 0:576], T.near[:], [R("NEI", 0, 576)], [], 5000)
    dma("Y", T.V[:, 4096:8192], T.rec[:, 4096:8192], [R("V", 4096, 8192)], [], 15000)
    dma("S", T.CIN[:], T.cen[:], [R("CIN")], [], 5000)
    dma("S", T.ABI[:, 512:1024], T.absorb[:, 512:1024], [R("ABI", 512, 1024)], [], 6000)

    PI = lambda k: R("PI", k, k + 1)
    CK = lambda k: R("CK", k, k + 1)
    r_, g_, fm, i14, i15, f32c, fNc, hc, r0, f16, fN16 = [CK(k) for k in range(11)]
    iota(PI(0), [[0, 1]], 1)
    iota(R("IOG"), [[1, 8], [0, 16]])
    iota(R("IOM"), [[0, 8], [1, 16]])
    iota(R("IOQ"), [[16, 8]])
    iota(R("IOJ"), [[1, 256]])
    iota(R("IOS"), [[16, 608]])
    for a in range(0, 4992, 1248):
        iota(R("TAB0", a, a + 1248), [[0, 1248]])
    node("V", lambda e: g.vector.tensor_scalar(ap(PI(1)), ap(PI(0)), 15, None, A.bitwise_and), [PI(1)], [PI(0)], 94)
    node("V", lambda e: g.vector.tensor_scalar(ap(PI(2)), ap(PI(0)), 4, None, A.arith_shift_right), [PI(2)], [PI(0)], 94)
    vc(r_, PI(1))
    vc(g_, PI(2))
    ts(fm, r_, 13.5, A.is_lt)
    ts(i14, r_, 14.0, A.is_equal)
    ts(i15, r_, 15.0, A.is_equal)
    ts(r0, r_, 0.0, A.is_equal)
    ts(hc, i14, 256.0, A.mult, i15, A.add)
    for c, v in ((f32c, 32.0), (fNc, -32.0), (f16, 16.0), (fN16, -16.0)):
        ts(c, fm, v, A.mult)
    ts(R("BD"), R("IOG"), g_, A.is_equal)
    fill(R("PL"), 0.0)
    for m in range(16):
        vc(R("PL", 128 * m + m, 128 * m + 128, 16), R("BD", m, 128, 16))
    for p, c in (("PLH", hc), ("PLF", f32c), ("PLN", fNc)):
        ts(R(p), R("PL"), c, A.mult)
    vc(R("POSTU", 0, 576), R("POSTI"))
    fill(R("POSTU", 576, 608), 0)
    vc(R("ABU", 0, 512), R("ABI", 0, 512))
    vc(R("ABU", 512, 1024), R("ABI", 512, 1024))
    ts(R("SLOT"), R("IOS"), r_, A.add)
    fill(R("REC", 8192, XW), 0.0)
    fill(R("ZER"), 0.0)
    ts(R("BDf"), R("IOG"), g_, A.is_equal)
    ts(R("D128"), R("IOM"), r_, A.is_equal)
    ts(R("D16"), R("IOM", 0, 16), r_, A.is_equal)
    ts(R("D16f"), R("IOM", 0, 16), r_, A.is_equal)
    x = ts(B(128), R("IOM"), r_, A.is_gt)
    tt(R("TRI"), R("BD"), x, A.mult)
    y = tt(B(128), R("BD"), R("D128"), A.mult)
    x = ts(B(128), R("TRI"), -256.0, A.mult)
    tt(R("WM"), x, y, A.add)
    ts(R("RL8"), R("IOQ"), 0.0, A.mult, r_, A.add)
    fill(R("LV", 576, PW), 0.0)
    for t in (0, 1):
        pc = 576 + 32 * t
        ts(CK(16 + 4 * t), r_, float(608 - pc), A.add)
        ts(CK(17 + 4 * t), r_, float(4864 + 16 * rank - 608 * rank - pc), A.add)
        ts(CK(18 + 4 * t), i14, float(36 + t), A.mult)
    ts(R("CV"), R("IOJ", 0, 128), 16.0, A.add, r0, A.mult)
    vc(R("POSTF", 0, 576), R("POSTI"))
    fill(R("POSTF", 576, 608), 0.0)
    ts(R("POSTF", 608, PW), R("IOJ", 0, 128), 8416.0, A.add, r0, A.mult)
    vc(R("NLU", 0, 576), R("NEI", 0, 576))
    fill(R("NLU", 576, 608), 0)
    fill(R("NEI", 576, PW), 0)
    ts(R("M30"), R("IOM", 0, 16), -2.0, A.mult, 30.0, A.add)
    ts(R("BW"), R("BD"), f16, A.mult)
    x = ts(F(128), R("IOM"), -1.0, A.mult, 15.0, A.add)
    y = ts(F(128), x, i14, A.mult, fN16, A.add)
    tt(R("CW"), y, R("BD"), A.mult)
    ts(R("R15"), R("BD"), i15, A.mult)
    ts(R("R15f"), R("BDf"), i15, A.mult)
    ts(R("BDm"), R("BD"), r_, A.mult)
    ts(R("RST"), R("IOJ", 0, 224), 0.0, A.is_gt)
    fill(R("RST", 0, 224, 16), 0.0)
    fill(R("ONE"), 1.0)
    x = ts(F(8), R("IOQ"), r_, A.add)
    ts(R("TC"), x, 16.0, A.add)
    ts(R("TCN"), R("TC"), -4096.0, A.mult)
    ts(R("NJC"), x, -1.0, A.mult)
    ts(R("C", 0, 576), R("CIN"), fm, A.mult, i14, A.add)
    ts(R("C", 576, PW), R("IOS", 0, 160), 0.0, A.mult, i14, A.add)
    for t in (0, 1):
        fill(R("BT%d" % t, 0, 16), 512.0)
        ts(R("HV%d" % t), R("IOJ"), i15, A.mult, CK(18 + 4 * t), A.add)
    fill(R("K1", 576, PW), 0.0)
    fill(R("ST", 576, PW), 0.0)
    fill(R("C255"), 255.0)
    ts(R("K16"), R("IOJ", 0, 16), 16.0, A.mult)
    x = ts(F(16), R("K16"), r_, A.add)
    ts(R("DM"), x, 8416.0, A.add)
    ts(CK(24), r_, 8544.0, A.add)
    fill(CK(25), -15.5)
    fill(R("X1", 8192, XW), 0.0)
    fill(R("X2", 8304, XW), 0.0)

    KEYQ = ["q0", "q1", "q0"]

    def absorb(X, Y, t, a, n):
        tt(R(Y, a, a + n), I(R(X, 0, 8416), R("ABU", 512 * t + a // 16, 512 * t + (a + n) // 16)), R("V", a, a + n), A.max)

    def gather(o, win, lst, a, b, e="VS"):
        for x in range(a, b, 56):
            y = min(b, x + 56)
            (act if e == "S" else either)(R(o, 16 * x, 16 * y), I(win, R(lst, x, y)))

    def live(c):
        a, b = CH[0][c]
        q = R(KEYQ[c], 0, b - a)
        spread(q, "PLH", lambda m: R("HG", 16 * a + m, 16 * b, 16), b - a)
        tt(R("LV", a, b), q, R("SLOT", a, b), A.is_equal)

    def count(t, c, S):
        a, b = CH[t][c]
        n = b - a
        q = R("q7", 0, n)
        mm(q, R("BD"), R("LV", a, b))
        fu = ts(B(n), q, 12.5, A.is_ge)
        scan(R("CUM", a, b), fu, R("ZER", 0, n), R("CUM", a - 1, a) if a else 0.0, A.add, A.add)
        le = ts(B(n), R("CUM", a, b), r_, A.is_le)
        red(cols(S["pc"], c, c + 1), le, A.add)

    def split(t, S):
        last = CH[t][2][1]
        inv = ts(F(1), R("CUM", last - 1, last), r_, A.is_le)
        pz = red(F(1), S["pc"], A.add)
        z = R("RZ%d" % t, 4 * rank, 4 * rank + 1)
        ts(z, inv, CK(17 + 4 * t), A.mult, pz, A.add)
        send_all(z, "mz%d" % t, z, [R("RZ%d" % t, 4 * s, 4 * s + 1) for s in range(8) if s != rank])
        plf = ts(F(1), inv, CK(16 + 4 * t), A.mult, pz, A.add)
        S["pl"] = ts(U(1), plf, float(-608 * rank), A.add)
        vc(R("LVN"), R("LV"))
        vc(I(R("LVN"), S["pl"]), R("ZER", 0, 16))

    def centres(t, X, S):
        pl = S["pl"]
        PS = S["PS"] = vc(FL(16), I(R("POSTF"), pl))
        LS = S["LS"] = vc(BL(16), I(R("LV"), pl))
        mm(R("q6", 0, 16), R("TRI"), LS)
        PSu = vc(U(16), PS)
        EXL = tt(B(128), I(LS, R("RL8")), R("BD"), A.mult)
        cz = ts(B(16), R("q6", 0, 16), 0.5, A.is_lt)
        mm(R("q7", 0, 16), EXL, R("D16"))
        oneA = tt(F(16), cz, LS, A.mult)
        XS = vc(BL(256), I(R(X), PSu))
        PRA = tt(F(16), oneA, PS, A.mult)
        mm(R("q6", 16, 32), R("BDf"), PRA)
        EXP = tt(F(128), I(PS, R("RL8")), R("BDf"), A.mult)
        rA = vc(U(16), R("q6", 16, 32))
        DA = tt(BL(256), I(R(X), rA), XS, A.subtract)
        LST = vc(FL(16), R("q7", 0, 16))
        mm(R("q7", 32, 48), EXP, R("D16f"))
        PST = vc(F(16), R("q7", 32, 48))
        AA = act(B(256), DA, AF.Abs)
        spread(R("q6", 32, 48), "PLF", lambda k: cols(AA, 16 * k, 16 * k + 16), 16)
        kb = tt(F(16), R("q6", 32, 48), R("M30"), A.add)
        kb = tt(F(16), kb, LST, A.mult)
        mx = red(F(1), kb, A.max)
        OB = ts(F(16), kb, mx, A.is_equal)
        rb = tt(F(16), OB, PST, A.mult)
        rB = red(FL(1), rb, A.add)
        rBu = vc(U(1), rB)
        bt = R("BT%d" % t, 16 + 16 * rank, 32 + 16 * rank)
        vc(bt, I(R(X), rBu))
        S["sent"] = send_all(bt, "mb%d" % t, bt, [R("BT%d" % t, 16 + 16 * s, 32 + 16 * s) for s in range(8) if s != rank])
        S["XS"], S["DA"], S["LST"], S["rB"], S["bt"] = XS, DA, LST, rB, bt
        S["dA"] = vc(FL(16), R("q6", 32, 48))

    def moved(t, X, S):
        PS, LS, XS, LST = S["PS"], S["LS"], S["XS"], S["LST"]
        dg = ts(F(16), R("D16f"), S["rB"], A.mult)
        mm(R("q6", 64, 80), R("BDf"), dg)
        rb = vc(U(16), R("q6", 64, 80))
        DB = tt(B(256), I(R(X), rb), XS, A.subtract)
        AB = act(B(256), DB, AF.Abs)
        spread(R("q6", 96, 112), "PLF", lambda k: cols(AB, 16 * k, 16 * k + 16), 16)
        go = tt(F(16), R("q6", 96, 112), S["dA"], A.is_lt)
        go = tt(B(16), go, LST, A.mult)
        EX = tt(B(128), I(go, R("RL8")), R("BD"), A.mult)
        mm(R("q6", 128, 144), EX, R("D16"))
        mm(R("q6", 160, 176), R("BD"), LS)
        goN = S["goN"] = vc(BL(16), R("q6", 128, 144))
        made = ts(F(16), R("q6", 160, 176), 0.5, A.is_gt)
        nf = ts(B(16), goN, -1.0, A.mult, 1.0, A.add)
        mm(R("q6", 192, 208), R("TRI"), nf)
        pf = tt(F(16), PS, made, A.mult)
        x = tt(F(16), PS, R("DM"), A.subtract)
        cf = ts(B(16), R("q6", 192, 208), 0.5, A.is_lt)
        x = tt(F(16), x, goN, A.mult)
        FR = S["FREE"] = tt(BL(16), cf, nf, A.mult)
        mm(R("q6", 224, 240), R("BDm"), FR)
        x = tt(F(16), x, R("DM"), A.add)
        pfr = tt(F(16), pf, FR, A.mult)
        mm(R("q6", 256, 272), R("BDf"), pfr)
        sl = vc(U(16), x)
        S["PNF"] = tt(FL(16), pf, pfr, A.subtract)
        w = tt(F(16), R("q6", 224, 240), R("K16"), A.add)
        pv = tt(F(16), R("q6", 256, 272), R("D16f"), A.mult)
        S["WV"] = ts(BL(16), w, i15, A.mult, CK(18 + 4 * t), A.add)
        pv = red(F(1), pv, A.add)
        S["CD"] = FL(16)
        ts(cols(S["CD"], 0, 1), pv, -1.0, A.mult, 9000.0, A.add)
        vc(I(R("REC"), sl), R("HV%d" % t))

    def table(t):
        zl = vc(U(8), R("RZ%d" % t, 0, 32, 4))
        vc(I(R("TAB%d" % t), zl), R("CV"))

    def target(t, c, S):
        a, b = CH[t][c]
        n = b - a
        spread(R("q2", 0, n), "PL", lambda m: R("HG", 16 * a + m, 16 * b, 16), n)
        x = either(B(n), R("q2", 0, n))
        mm(R("q3", 0, n), R("WM"), x)
        u = ts(B(n), R("q3", 0, n), 0.0, A.max)
        spread(R("q3", 448, 448 + n // 16), "PL", lambda m: cols(u, m, n, 16), n // 16)
        mm(R("q3", 224, 224 + n), R("BD"), u)
        tu = vc(U(n // 16), R("q3", 448, 448 + n // 16))
        S["tg%d" % c] = either(BL(n), R("q3", 224, 224 + n))
        S["b%d" % c] = act(BL(n), I(R("BT%d" % t), tu))

    def gains(t, c, S):
        a, b = CH[t][c]
        n = b - a
        q = R(KEYQ[c], 0, n)
        mm(q, R("CW"), R("C", a, b), True, False)
        act(R("q5", 0, n), R("C", a, b))
        for m in range(16):
            o = R("MC%d" % (c % 2), m * n, m * n + n)
            tt(o, R("V", 16 * a + m, 16 * b, 16), R("q5", 0, n), A.max)
            mm(q, R("PLF", 128 * m, 128 * m + 128), o, False, False)
        act(R("q4", 0, n), S["b%d" % c])
        mm(q, R("BW"), S["b%d" % c], False, False)
        for m in range(16):
            o = R("MB%d" % (c % 2), m * n, m * n + n)
            tt(o, R("V", 16 * a + m, 16 * b, 16), R("q4", 0, n), A.max)
            mm(q, R("PLN", 128 * m, 128 * m + 128), o, False, m == 15)

    def best(t, c, S):
        a, b = CH[t][c]
        n = b - a
        tt(R("K1", a, b), R(KEYQ[c], 0, n), R("LVN", a, b), A.mult)
        kt = turn(R("KT", 0, n), R("K1", a, b))
        sc = scan(R("SG", 0, n), R("RST", 0, n), kt, 0.0, A.mult, A.max)
        turn(R("ST", a, b), sc)
        of = act(B(n), R("ST", a, b), AF.Sign, bias=CK(25))
        mm(R("q7", 0, n), R("R15"), of)
        tg = tt(B(n), R("q7", 0, n), S["tg%d" % c], A.mult)
        QS = [0, 1, 2, 3] if c == 2 else [0, 1, 2, 3, 4, 5, 6, 7]
        for q in range(8):
            o, s = R("E", q * n, q * n + n), R("SC", q * n, q * n + n)
            if q in QS:
                act(o, tg, AF.Abs, bias=R("TCN", q, q + 1), scale=4096.0)
            else:
                ts(o, tg, R("TC", q, q + 1), A.not_equal, 4096.0, A.mult)
            scan(s, o, R("ONE", 0, n), 4096.0, A.min, A.subtract)
        x = ts(F(8), R("SC", n - 1, 8 * n, n), -1.0, A.mult, float(608 - b), A.add)
        S["G"] = tt(FL(8), x, S["G"], A.max)

    def movers(t, X, S):
        arr = "ARR%d" % t
        ql = ts(U(8), S["G"], -1.0, A.mult, 608.0, A.add)
        val = ts(FL(8), S["G"], 0.5, A.is_gt)
        fill(R("RV%d" % t, 4 * rank, 4 * rank + 1), 0.0)
        send_each(lambda d: cols(val, T.rank_of(d), T.rank_of(d) + 1), "mv%d" % t, lambda d: R("RV%d" % t, 4 * rank, 4 * rank + 1),
                  [R("RV%d" % t, 4 * s, 4 * s + 1) for s in range(8) if s != rank])
        st = vc(F(128), I(R("ST"), ql))
        mm(R("q7", 0, 128), R("R15f"), st)
        k1 = vc(F(128), I(R("K1"), ql))
        pm = vc(F(128), I(R("POSTF"), ql))
        OB = tt(BL(128), k1, R("q7", 0, 128), A.is_equal)
        pr = tt(F(128), OB, pm, A.mult)
        mm(R("q7", 128, 256), R("BDf"), pr)
        dd = tt(F(128), R("q7", 128, 256), R("D128"), A.mult)
        sc = scan(FL(128), R("RST", 0, 128), dd, 0.0, A.mult, A.max)
        idl = vc(U(8), cols(sc, 15, 128, 16))
        MV = vc(BL(128), I(R(X), idl))
        send_each(lambda d: cols(MV, 16 * T.rank_of(d), 16 * T.rank_of(d) + 16), "ma%d" % t,
                  lambda d: (lambda o: R(arr, 16 * o, 16 * o + 16))(rank if rank < T.rank_of(d) else rank - 1), [R(arr)])
        S["ql"], S["OB"], S["val"] = ql, OB, val
        S["own"] = cols(sc, 16 * rank + 15, 16 * rank + 16)
        vc(I(R("REC"), idl), R("C255"))

    def winner(t, S):
        RV, CD = "RV%d" % t, S["CD"]
        tab = FL(8)
        fill(tab, 0.0)
        for s in range(8):
            if s != rank:
                ts(cols(tab, s, s + 1), r_, -1.0, A.mult, float(20000 - 8192 - (7 * t + (s if s < rank else s - 1)) * 16), A.add)
        ow = ts(F(1), S["own"], -1.0, A.mult, 30000.0, A.add)
        tt(cols(CD, 1, 2), ow, cols(S["val"], rank, rank + 1), A.mult)
        tt(cols(CD, 2, 10), R(RV, 0, 32, 4), tab, A.mult)
        c = red(F(1), cols(CD, 0, 10), A.max)
        hw = ts(F(1), c, 10000.0, A.is_gt)
        b1 = ts(F(1), c, 20500.0, A.is_gt, 10000.0, A.mult)
        w = ts(F(1), hw, 11000.0, A.mult, c, A.subtract)
        w = ts(F(1), w, b1, A.add, 9000.0, A.add)
        dg = F(32)
        ts(cols(dg, 0, 16), R("D16f"), w, A.mult)
        ts(cols(dg, 16, 32), R("D16f"), hw, A.mult)
        mm(R("q7", 288, 320), R("BDf"), dg)
        x = ts(F(1), w, CK(24), A.subtract, hw, A.mult)
        wl = ts(U(1), x, CK(24), A.add)
        f = tt(F(16), S["FREE"], R("q7", 288, 304), A.mult)
        n = 576 + 16 * t
        tt(R("POSTF", n, n + 16), f, S["PNF"], A.add)
        if t == 0:
            f = tt(B(16), S["FREE"], R("q7", 304, 320), A.mult)
            tt(R("LV", n, n + 16), f, S["goN"], A.add)
            vc(R("POSTU", n, n + 16), R("POSTF", n, n + 16))
        vc(I(R("REC"), wl), S["WV"])

    def update(S):
        pl = S["pl"]
        ls = tt(B(16), S["LS"], S["goN"], A.subtract)
        vc(I(R("LV"), pl), ls)
        lm = vc(B(128), I(R("LV"), S["ql"]))
        lm = tt(B(128), lm, S["OB"], A.subtract)
        lm = ts(B(128), lm, 0.0, A.max)
        vc(I(R("LV"), S["ql"]), lm)
        at = tt(B(16), cols(S["DA"], 0, 256, 16), cols(S["XS"], 0, 256, 16), A.add)
        at = ts(B(16), at, fm, A.mult, i14, A.add)
        vc(I(R("C"), pl), at)
        ts(R("C", 576, 592), S["bt"], fm, A.mult, i14, A.add)
        vc(R("NLU", 576, 592), I(R("NEI"), pl))

    SS = [{"pc": FL(4), "G": R("NJC")}, {"pc": FL(4), "G": R("NJC")}]
    for t in (0, 1):
        S, X, W = SS[t], "X2" if t else "X1", "X1" if t else "REC"
        fill(cols(S["pc"], 3, 4), float(608 * rank))
        if t == 0:
            for c in range(3):
                gather("HG", R("REC", 0, 8192), "POSTU", CH[0][c][0], CH[0][c][1], "S")
                live(c)
                count(0, c, S)
        else:
            for c in range(3):
                count(1, c, S)
        split(t, S)
        if t:
            vc(R("X1", 8192, 8304), R("ARR0"))
            vc(R("X2", 8192, 8304), R("ARR0"))
            for a in (0, 4096):
                dma("Y", T.V[:, a:a + 4096], T.X1[:, a:a + 4096], [R("V", a, a + 4096)], [R("X1", a, a + 4096)], 5500)
        for a in range(0, 8192, 2048):
            absorb(W, X, t, a, 2048)
        if t == 0:
            fill(R("REC", 8192, 8416), 255.0)
        centres(t, X, S)
        if t == 0:
            for a in range(0, 4992, 1248):
                iota(R("TAB1", a, a + 1248), [[0, 1248]], 0, [S["sent"]])
        moved(t, X, S)
        table(t)
        for c in range(3):
            gather("HG", R("TAB%d" % t), "NLU", *CH[t][c])
        for c in range(3):
            gather("V", R(X, 0, 8304) if t else R(X, 0, 8192), "POSTU", *CH[t][c])
        for c in range(3):
            target(t, c, S)
        for c in range(3):
            gains(t, c, S)
            best(t, c, S)
        movers(t, X, S)
        if t == 0:
            update(S)
        winner(t, S)
    dma("Y", T.ypost[:], T.POSTF[:, 0:608], [], [R("POSTF", 0, 608)], 3000)
    for k in range(8):
        dma("YS"[k % 2], T.yh[2 * k:2 * k + 2, :], T.REC[16 * k + 14:16 * k + 16, 0:8192], [], [R("REC", 0, 8192)], 3000)
    y = ts(B(224), R("REC", 8192, 8416), fm, A.mult)
    h = tt(B(224), R("REC", 8192, 8416), y, A.subtract)
    y = B(224)
    ts(cols(y, 0, 112), R("ARR0"), fm, A.mult)
    ts(cols(y, 112, 224), R("ARR1"), fm, A.mult)
    ya = tt(B(224), y, h, A.add)
    dma("Y", T.ya[:], ap(ya), [], [ya], 2500)
    emit()
